import numpy as np, ml_dtypes
CORES = [48,51,52,55]
N = 4
BF = ml_dtypes.bfloat16
def gentries(a):
    return np.ascontiguousarray(a.reshape(8, 16, -1).transpose(0, 2, 1)).reshape(8, -1)
def gtable(e):
    e = np.asarray(e); return np.ascontiguousarray(e.reshape(8, -1, 16).transpose(0, 2, 1)).reshape(128, -1).astype(np.int32)
V, A, VIS, ST = 3840, 256, 3, 4
def order(rng):
    return np.argsort(rng.random((N, 8, V)), axis=-1)
def by_order(o, ix):
    n = np.take_along_axis(o, ix.reshape(N, 8, V * 16), 2).reshape(N, 8, V, 16); b = np.empty_like(n)
    np.put_along_axis(b, o[..., None], n, 2)
    return b
def parts(rng):
    o = order(rng); i = np.arange(V)[None, None, :, None]; sh = (N, 8, V, 16)
    near = (i + rng.integers(-12, 13, sh)) % V; far = np.minimum((V * rng.random(sh) ** 2).astype(np.int64), V - 1)
    nm = by_order(o, np.where(rng.random(sh) < 0.5, near, far))
    return nm, rng.integers(0, 16, (N, 8, 16, V)), rng.integers(0, V, (N, 8, A)), rng.integers(0, 16, (N, 8, 16, A)), rng.integers(0, 32, (N, 8, 16, A))
def pack(nm, x, v, z, nz):
    return {"adj": np.stack([gtable(a.reshape(8, -1)) for a in nm]), "x": x.reshape(N, 128, V).astype(np.float32).astype(BF), "v0": np.stack([gtable(a) for a in v]),
            "z": z.reshape(N, 128, A).astype(np.float32).astype(BF), "nz": nz.reshape(N, 128, A).astype(np.float32).astype(BF)}
def setup_inputs(rng):
    return pack(*parts(rng))
def setup_inputs_loops(rng):
    nm, x, v, z, nz = parts(rng); o = order(rng); i = np.arange(V)[None, None, :]; m = ST + 1
    chain = np.where(i % m == m - 1, i - i % m + rng.integers(0, m, (N, 8, V)), (i + 1) % V)
    c = rng.integers(2, 3 * ST, (N, 8, 1)); base = i - i % c
    circle = np.minimum(base[..., None] + (rng.random((N, 8, V, 16)) * c[..., None]).astype(np.int64), V - 1)
    odd = (np.arange(8) % 2 == 1)[None, :, None, None]
    nm = by_order(o, np.where(odd, circle, chain[..., None]))
    alike = np.take_along_axis(x, np.take_along_axis(o, base, 2)[:, :, None, :], 3); y = np.empty_like(x)
    np.put_along_axis(y, o[:, :, None, :], alike, 3)
    return pack(nm, np.where(odd, y, x), v, z, nz)
def setup_inputs_crowd(rng):
    nm, x, v, z, nz = parts(rng); h = 12
    hub = 1 + np.argsort(rng.random((8, V - 2)), axis=-1)[:, :h]; hub[:, 0] = 0; hub[:, 1] = V - 1
    for g in range(6):
        for q in range(N):
            nm[q, g, hub[g]] = hub[g][rng.integers(0, h, (h, 16))]
        v[:, g] = hub[g][rng.integers(0, h, (N, A))]
    for q in range(N):
        p = rng.permutation(h); nm[q, 5, hub[5][p], 3] = hub[5][np.roll(p, -1)]
    x[:, 5] = x[:, 5, :, :1]; nz[:, 5] = 0; nz[:, 5, 3] = 31
    v[:, 6] = V - 1; v[:, 7] = 0
    return pack(nm, x, v, z, nz)
def setup_inputs_ties(rng):
    nm, x, v, z, nz = parts(rng)
    x[:, :2] = 7 + x[:, :2] % 2; z[:, :2] = 7 + z[:, :2] % 2; nz[:, :2] = nz[:, :2] % 2
    x[:, 2:4] = 15 * (x[:, 2:4] % 2); z[:, 2:4] = 15 * (z[:, 2:4] % 2); nz[:, 2:4] = 0
    v[:, 2, 0] = 0; nm[:, 2, 0] = V - 1; x[:, 2, :, V - 1] = 15; z[:, 2, :, 0] = 0
    x[:, 4] = 5; nz[:, 4] = 30 + nz[:, 4] % 2
    x[:, 5] = x[:1, 5]; nm[:, 5] = nm[:1, 5]; nz[:, 5] = 0
    nm[:, 6] = np.tile(nm[:, 6, :, :2], (1, 1, 8)); nz[:, 6] = nz[:, 6] % 4
    nz[:, 7] = 31
    return pack(nm, x, v, z, nz)
def setup_inputs_ends(rng):
    nm, x, v, z, nz = parts(rng)
    x[:, 0] = 15 - (x[:, 0] == 0).astype(np.int64); z[:, 0] = 0; nz[:, 0] = nz[:, 0] % 2
    x[:, 4] = (x[:, 4] == 0).astype(np.int64); z[:, 4] = 15; nz[:, 4] = nz[:, 4] % 4
    x[:, 1] = 7 + (x[:, 1] == 0).astype(np.int64); z[:, 1] = 7; nz[:, 1] = 24 + nz[:, 1] % 8
    level = ((int(rng.integers(0, N)) - np.arange(N)) % N)[:, None, None]
    x[:, 2] = 2 * level + x[:, 2] % 2; x[:, 3] = 2 * level; z[:, 2:4] = 0
    i = np.arange(V)[None, None, :, None]
    nm[:, 2:4] = by_order(order(rng), (i + 1 + rng.integers(0, 13, (N, 8, V, 16))) % V)[:, 2:4]
    v[:, 2:4] = np.argsort(rng.random((N, 2, V)), axis=-1)[..., :A]; v[:, 3, A - 1] = v[:, 3, 0]
    nz[:, 3] = nz[:, 3] % 31
    for q in range(N):
        k = int(rng.integers(0, 16)); nz[q, 3, k, 0] = 31; nz[q, 3, (k + 1 + int(rng.integers(0, 15))) % 16, A - 1] = 31
    return pack(nm, x, v, z, nz)
def setup_inputs_spread(rng):
    nm, x, v, z, nz = parts(rng); e = np.array([0.5, 1.0, 2.0, 4.0])
    ix = np.minimum(np.exp2(np.log2(V) * rng.random((N, 8, V, 16))).astype(np.int64) - 1, V - 1)
    nm = by_order(order(rng), ix); nm[:, 1::2] = V - 1 - ix[:, 1::2]
    x = np.minimum((16 * rng.random(x.shape) ** rng.choice(e, (N, 8, 1, V))).astype(np.int64), 15)
    z = np.minimum((16 * rng.random(z.shape) ** rng.choice(e, (N, 8, 1, A))).astype(np.int64), 15)
    nz = np.minimum((32 * rng.random(nz.shape) ** rng.choice(e, (N, 8, 16, 1))).astype(np.int64), 31)
    v = np.minimum((V * rng.random(v.shape) ** rng.choice(e, (N, 8, 1))).astype(np.int64), V - 1)
    return pack(nm, x, v, z, nz)
def check_inputs(d):
    bad = []
    for k, hi in (("adj", V - 1), ("v0", V - 1)):
        if np.min(d[k]) < 0 or np.max(d[k]) > hi: bad.append("range of " + k)
    for k, hi in (("x", 15), ("z", 15), ("nz", 31)):
        b = np.asarray(d[k]).astype(np.float32)
        if not np.all((b >= 0) & (b <= hi) & (b == np.floor(b))): bad.append("whole numbers of " + k)
    return bad
def reference(adj, x, v0, z, nz):
    nm = np.stack([gentries(b) for b in adj]).astype(np.int64).reshape(N, 8, V, 16)
    xt = np.ascontiguousarray(x.astype(np.float32).astype(np.int32).reshape(N, 8, 16, V).transpose(0, 1, 3, 2))
    w = np.ascontiguousarray(z.astype(np.float32).astype(np.int32).reshape(N, 8, 16, A).transpose(0, 1, 3, 2))
    no = np.ascontiguousarray(nz.astype(np.float32).astype(np.int64).reshape(N, 8, 16, A).transpose(0, 1, 3, 2))
    v = np.stack([gentries(b) for b in v0]).astype(np.int64)
    ph = np.full((N, 8, V, 16), 8, np.int64)
    r = np.arange(N)[:, None, None]; g = np.arange(8)[None, :, None]; pl = np.arange(ST)
    oldn = oldk = oldd = None
    for i in range(VIS):
        if i > 0: v = np.roll(v, 1, axis=0); w = np.roll(w, 1, axis=0)
        tn = np.full((N, 8, A, ST), -1, np.int64); tk = np.zeros((N, 8, A, ST), np.int64); ln = np.zeros((N, 8, A), np.int64)
        for s in range(ST):
            names = nm[r, g, v]
            far = np.sum(np.abs(xt[r[..., None], g[..., None], names] - w[:, :, :, None, :]), axis=4)
            k = np.argmax(ph[r, g, v] + np.roll(no, -(i * ST + s), axis=2) - far, axis=3)
            nv = np.take_along_axis(names, k[..., None], 3)[..., 0]
            here = pl == ln[..., None]
            tn = np.where(here, v[..., None], tn); tk = np.where(here, k[..., None], tk)
            hit = tn == nv[..., None]
            ln = np.where(np.any(hit, axis=3), np.argmax(hit, axis=3), ln + 1)
            tn = np.where(pl < ln[..., None], tn, -1); v = nv
        dd = np.sum(np.abs(xt[r, g, v] - w), axis=3)
        if i > 0:
            better = np.roll(dd < np.roll(oldd, 1, axis=0), -1, axis=0)
            for p in range(ST):
                q, h, b = np.nonzero(better & (oldn[..., p] >= 0))
                n = oldn[q, h, b, p]; kk = oldk[q, h, b, p]
                low = np.full((N, 8, V), A, np.int64); np.minimum.at(low, (q, h, n), b)
                m = low[q, h, n] == b; q, h, n, kk = q[m], h[m], n[m], kk[m]
                was = ph[q, h, n]; now = np.maximum(was - 3, 0); j = np.arange(len(q))
                now[j, kk] = np.minimum(was[j, kk] + 8, 20)
                ph[q, h, n] = now
        oldn, oldk, oldd = tn, tk, dd
    return {"yp": ph.transpose(0, 1, 3, 2).reshape(N, 128, V).astype(np.float32).astype(BF), "yv": np.stack([gtable(b) for b in v]).astype(np.float32)}

@@ -1,0 +1,443 @@
+from concourse.mybir import AluOpType as A, ActivationFunctionType as F
+
+NPOS = [(2, 2)] * 4 + [(3, 3)] * 4 + [(8, 8)] + [(4, 4)] * 3
+FR, FG, FB, KEEP = (20, 8), 1, (12, 0), (30, 22)
+BANK = [("cn0", 0), ("cn1", 0), ("cn1", 256), ("cn2", 0)]
+CLAIM = 65536.0
+BF, FH, F4, I4, U2 = "bfloat16", "float16", "float32", "int32", "uint16"
+SCRATCH = {n: ("sbuf", [128] + s, d) for n, s, d in [
+    ("adjw", [3840], I4), ("xw", [3840], BF), ("phw", [4096], BF), ("v0t", [16], I4), ("zt", [256], BF), ("nzt", [256], BF),
+    ("zp", [8, 2, 16], BF), ("nzp", [8, 2, 16], BF), ("nzq", [8, 32], BF), ("nts", [272], BF),
+    ("zz0", [4096], BF), ("zz1", [4096], BF), ("zz2", [4096], BF), ("off", [208], U2), ("offi1", [16], U2), ("offi2", [16], U2),
+    ("ones", [8, 16], BF), ("bm", [8, 16], BF), ("idn", [8, 16], BF), ("idm", [128], BF), ("onesh", [128], FH), ("kcf", [128], F4),
+    ("kc", [128], FH), ("bsl", [144], BF), ("ef", [4, 4, 2, 16], FH), ("eb", [4, 128], BF), ("sh", [22, 128], BF),
+    ("rst", [128], F4), ("rsp", [512], F4), ("iw", [4096], I4), ("rri", [2], I4), ("rrf", [2], F4), ("dum", [64], F4),
+    ("dlt", [16], F4), ("pen", [32, 16], BF), ("dwin", [16], BF), ("mw", [16], F4), ("rowi", [16], F4), ("dg", [256], BF),
+    ("da", [16, 16], BF), ("ds0", [16], F4), ("ds1", [16], F4), ("ds2", [16], F4), ("din1", [16], F4), ("din2", [16], F4),
+    ("bet", [16], F4), ("bt", [16, 128], BF), ("ee", [4, 80], F4), ("al", [64], F4), ("hh", [64], F4), ("pl", [64], F4),
+    ("na", [64], F4), ("cod", [64], F4), ("ww", [4, 64], F4), ("w2", [4, 4, 16], F4), ("w3", [4, 2, 16], F4), ("cp", [4, 16], F4),
+    ("ci", [64], I4), ("nx", [64], F4), ("kv", [64], I4), ("scn", [768], F4), ("okm", [48], F4), ("ofl", [64], U2),
+    ("t1", [256], BF), ("t2", [256], BF), ("yvt", [16], F4), ("yvi", [16], I4), ("hi2", [64], I4)]}
+SCRATCH.update({n: ("psum", [128, 512], F4) for n in ("fb0", "fb1", "ps0", "ps1", "cn0", "cn1", "cn2", "pm")})
+for _h in "01":
+    SCRATCH.update({n + _h: ("sbuf", [128] + s, d) for n, s, d in [
+        ("nm", [128], U2), ("nf", [128], FH), ("nt", [4, 32], FH), ("pb", [128], BF), ("pt", [4, 32], BF), ("dr", [2048], BF),
+        ("aa", [128, 16], BF), ("xr", [2048], BF), ("sc", [128], F4), ("ni", [8], I4), ("hi", [64], I4), ("nv", [80], I4),
+        ("uf", [64], F4), ("ud", [64], F4), ("ul", [64], U2), ("kl", [64], U2), ("dl", [1024], BF), ("ubc", [1024], U2),
+        ("eq", [64, 128], BF)]})
+SEMAPHORES = ["sv", "ss", "sp", "sg", "la0", "la1", "lx", "lz", "ln", "lv", "oy0", "oy1", "ov"]
+SEMAPHORES += [a + b for a in "rt" for b in ("z1", "z2", "o10", "o11", "o20", "o21", "d1", "d2")]
+
+
+def rank_program(g, core, T, topo):
+    rank = T.rank_of(core)
+    if rank is None:
+        return
+    ENG = {"V": g.vector, "S": g.scalar, "P": g.tensor, "G": g, "Y": g.sync}
+    OWN = {"V": "sv", "S": "ss", "P": "sp", "G": "sg"}
+    V, S, P = g.vector, g.scalar, g.tensor
+    cnt, snap, writes, reads = {}, {}, {}, {}
+    clk = {e: {} for e in ENG}
+
+    def need(e, tok):
+        sem, val = tok
+        c = clk[e]
+        if c.get(sem, 0) >= val:
+            return
+        ENG[e].wait_ge(T.sem[sem], val)
+        c[sem] = val
+        for k, v in snap.get(tok, {}).items():
+            if c.get(k, 0) < v:
+                c[k] = v
+
+    def hits(d, b, lo, hi):
+        return [x for x in d.get(b, []) if x[0] < hi and lo < x[1]]
+
+    def op(e, make, w=(), r=(), sem=None, inc=1):
+        deps = {}
+
+        def dep(tok):
+            if deps.get(tok[0], 0) < tok[1]:
+                deps[tok[0]] = tok[1]
+        for k, regs in enumerate((r, w)):
+            for b, lo, hi in regs:
+                for x in hits(writes, b, lo, hi):
+                    if not (e == "P" and x[3] == "P"):
+                        dep(x[2])
+                if k or SCRATCH[b][0] == "psum":
+                    for x in hits(reads, b, lo, hi):
+                        if x[3] != e:
+                            dep(x[2])
+        for tok in sorted(deps.items(), key=lambda t: -t[1]):
+            need(e, tok)
+        ins = make()
+        s = sem or OWN[e]
+        if ins is not None:
+            ins.then_inc(T.sem[s], inc)
+        cnt[s] = cnt.get(s, 0) + inc
+        tok = (s, cnt[s])
+        snap[tok] = dict(clk[e])
+        who = e if sem is None else "dma"
+        for b, lo, hi in w:
+            writes[b] = [x for x in writes.get(b, []) if not (lo <= x[0] and x[1] <= hi)] + [(lo, hi, tok, who)]
+            reads[b] = [x for x in reads.get(b, []) if not (lo <= x[0] and x[1] <= hi)]
+        for b, lo, hi in r:
+            reads[b] = [x for x in reads.get(b, []) if not (x[3] == who and lo <= x[0] and x[1] <= hi)] + [(lo, hi, tok, who)]
+
+    def al(b):
+        return (b, 0, 1 << 20)
+
+    def vop(f, w, r):
+        op("V", f, w, r)
+
+    def mm(*a):
+        return lambda: P.matmul(*a)
+
+    HU = [(h, u) for h in range(2) for u in range(2)]
+    op("Y", lambda: g.sync.dma_start(T.zt[:], T.z[:]), [al("zt")], [], "lz", 16)
+    op("S", lambda: g.scalar.dma_start(T.v0t[:], T.v0[:]), [al("v0t")], [], "lv", 16)
+    op("S", lambda: g.scalar.dma_start(T.nzt[:], T.nz[:]), [al("nzt")], [], "ln", 16)
+    op("Y", lambda: g.sync.dma_start(T.adjw[:, 0:1920], T.adj[:, 0:1920]), [("adjw", 0, 1920)], [], "la0", 16)
+    op("S", lambda: g.scalar.dma_start(T.adjw[:, 1920:3840], T.adj[:, 1920:3840]), [("adjw", 1920, 3840)], [], "la1", 16)
+    op("Y", lambda: g.sync.dma_start(T.xw[:], T.x[:]), [al("xw")], [], "lx", 16)
+    vop(lambda: V.memset(T.ones[:], 1.0), [al("ones")], [])
+    vop(lambda: V.memset(T.ef[:], 0.0), [al("ef")], [])
+    vop(lambda: V.memset(T.onesh[:], 1.0), [al("onesh")], [])
+    op("G", lambda: g.affine_select(T.bm[:], T.ones[:], [[-16, 8], [0, 16]], A.is_ge, 0.0, 0, 1), [al("bm")], [al("ones")])
+    op("G", lambda: g.affine_select(T.bm[:], T.bm[:], [[16, 8], [0, 16]], A.is_ge, 0.0, 15, -1), [al("bm")], [al("bm")])
+    op("G", lambda: g.iota(T.kcf[:], [[0, 8], [-32, 16]], 495, 0, allow_small_or_imprecise_dtypes=True), [al("kcf")], [])
+    for u, w in HU:
+        i = 2 * u + w
+        op("G", lambda: g.affine_select(T.ef[:, i, :, w, :], T.onesh[:, 0:64], [[32, 4], [1, 16]], A.is_equal, 0.0, 16 * u, -1),
+           [("ef", 128 * i, 128 * i + 128)], [al("onesh")])
+    op("G", lambda: g.affine_select(T.idn[:], T.ones[:], [[16, 8], [1, 16]], A.is_equal, 0.0, 0, -1), [al("idn")], [al("ones")])
+    for h, u in HU:
+        vop(lambda: V.tensor_copy(T.zp[:, 4 * h:4 * h + 4, u, :], T.zt[:, 128 * h + 64 * u:128 * h + 64 * u + 64]), [("zp", 2 * h + u, 2 * h + u + 1)], [al("zt")])
+    for k in range(16):
+        vop(lambda: V.tensor_copy(T.zz0[:, k::16], T.zp[:]), [("zz0", k, k + 1)], [al("zp")])
+    writes["zz0"] = [(0, 1 << 20, ("sv", cnt["sv"]), "V")]
+    vop(lambda: V.memset(T.rst[:], 0.0), [al("rst")], [])
+    vop(lambda: V.memset(T.rst[:, 0::16], -1.0e9), [al("rst")], [])
+    vop(lambda: V.memset(T.bsl[:], 0.0), [al("bsl")], [])
+    vop(lambda: V.tensor_scalar(T.bsl[:, 15:128:16], T.bm[:, :, 0], -CLAIM, None, A.mult), [al("bsl")], [al("bm")])
+    vop(lambda: V.tensor_copy(T.kc[:], T.kcf[:]), [al("kc")], [al("kcf")])
+    vop(lambda: V.tensor_scalar(T.eb[:], T.ef[:], CLAIM, None, A.mult), [al("eb")], [al("ef")])
+    vop(lambda: V.tensor_scalar(T.idm[:], T.idn[:], -1.0, None, A.mult), [al("idm")], [al("idn")])
+    vop(lambda: V.memset(T.phw[:], 8.0), [al("phw")], [])
+    for h, u in HU:
+        vop(lambda: V.tensor_copy(T.off[:, 8 * h + u:8 * h + 8:2], T.v0t[:, 8 * h + 4 * u:8 * h + 4 * u + 4]), [("off", 8 * h + 4 * u, 8 * h + 4 * u + 4)], [al("v0t")])
+    for h, u in HU:
+        op("S", lambda: S.activation(T.nzp[:, 4 * h:4 * h + 4, u, :], T.nzt[:, 128 * h + 64 * u:128 * h + 64 * u + 64], F.Copy), [("nzp", 2 * h + u, 2 * h + u + 1)], [al("nzt")])
+    vop(lambda: V.transpose(T.nzq[:], T.nzp[:]), [al("nzq")], [al("nzp")])
+    for h, u in HU:
+        for w in range(2):
+            op("P", mm(T.pm[:, 128 * h + 64 * u:128 * h + 64 * u + 64], T.eb[:, 2 * u + w, :], T.nzq[:, 4 * h:4 * h + 4, 16 * w:16 * w + 16], w == 0, w == 1),
+               [al("pm")], [al("eb"), al("nzq")])
+    op("S", lambda: S.activation(T.nts[:, 0:256], T.pm[:, 0:256], F.Copy), [("nts", 0, 256)], [al("pm")])
+    op("S", lambda: S.activation(T.nts[:, 256:272], T.pm[:, 0:16], F.Copy), [("nts", 256, 272)], [al("pm")])
+
+    def send(dst, out, src, name, srcreg, landreg):
+        m, n = topo.mask(core, dst), len(topo.engines(core, dst))
+        rid, pid, _ = topo.addr(dst)
+
+        def make():
+            g.remote_dma(out, src, T.sem["r" + name], T.sem["t" + name], pid, rid, m)
+        op("G", make, [], [srcreg], "t" + name, n)
+        cnt["r" + name] = n
+        writes.setdefault(landreg[0], []).append((landreg[1], landreg[2], ("r" + name, n), "rem"))
+
+    nxt, nx2, prv = (T.cores[(rank + d) % 4] for d in (1, 2, 3))
+    send(nxt, T.zz1[:], T.zz0[:], "z1", al("zz0"), al("zz1"))
+    for t in range(1, 12):
+        for y in range(2):
+            i = 2 * (t - 1) + y
+            op("G", lambda: g.affine_select(T.sh[:, i, :], T.bm[:], [[-16, 8], [-1, 16]], A.is_equal, 0.0, 16 * y - t, 1), [("sh", i, i + 1)], [al("bm")])
+        if t == 4:
+            send(nx2, T.zz2[:], T.zz0[:], "z2", al("zz0"), al("zz2"))
+            op("G", lambda: g.iota(T.iw[:], [[1, 4096]], 0, 0), [al("iw")], [])
+            op("G", lambda: g.iota(T.rri[:], [[0, 2]], 0, 1), [al("rri")], [])
+            op("G", lambda: g.iota(T.dum[:], [[0, 4], [16, 16]], 3840, 0, allow_small_or_imprecise_dtypes=True), [al("dum")], [])
+            op("G", lambda: g.iota(T.rowi[:], [[1, 16]], 0, 0, allow_small_or_imprecise_dtypes=True), [al("rowi")], [])
+
+    def late_constants():
+        L = []
+
+        def c(f, w, r):
+            L.append(lambda: vop(f, w, r))
+        c(lambda: V.tensor_scalar(T.rri[:], T.rri[:], 15, None, A.bitwise_and), [al("rri")], [al("rri")])
+        c(lambda: V.tensor_copy(T.rrf[:], T.rri[:]), [al("rrf")], [al("rri")])
+        c(lambda: V.tensor_scalar(T.dum[:], T.dum[:], T.rrf[:, 0:1], None, A.add), [al("dum")], [al("dum"), al("rrf")])
+        c(lambda: V.tensor_scalar(T.dwin[:], T.rowi[:], T.rrf[:, 0:1], None, A.is_equal), [al("dwin")], [al("rowi"), al("rrf")])
+        c(lambda: V.tensor_scalar(T.mw[:], T.rowi[:], T.rrf[:, 0:1], None, A.is_gt), [al("mw")], [al("rowi"), al("rrf")])
+        c(lambda: V.tensor_scalar(T.dlt[:], T.dwin[:], 0.5, None, A.mult), [al("dlt")], [al("dwin")])
+        c(lambda: V.tensor_tensor(T.mw[:], T.mw[:], T.dlt[:], A.add), [al("mw")], [al("mw"), al("dlt")])
+        c(lambda: V.tensor_scalar(T.pen[:, 0, :], T.dwin[:], -1024.0, 1024.0, A.mult, A.add), [("pen", 0, 1)], [al("dwin")])
+        c(lambda: V.tensor_scalar(T.dwin[:], T.dwin[:], 11.0, -3.0, A.mult, A.add), [al("dwin")], [al("dwin")])
+        for n in (1, 2, 4, 8, 16):
+            c(lambda n=n: V.tensor_copy(T.pen[:, n:2 * n, :], T.pen[:, 0:n, :]), [("pen", n, 2 * n)], [("pen", 0, n)])
+        c(lambda: V.memset(T.rsp[:], 0.0), [al("rsp")], [])
+        c(lambda: V.memset(T.rsp[:, 0::16], 1.0e6), [al("rsp")], [])
+        return L
+
+    fbn = [0]
+
+    def table(t, h):
+        return ("offi%d" % (t // 4), 8 * h) if t % 4 == 0 and t > 0 else ("off", 16 * t + 8 * h)
+
+    def p_gather(t, h):
+        on, lo = table(t, h)
+        op("S", lambda: S.activation(T["pb%d" % h][:], T.phw[:, 0:3840].indirect(T[on][:, lo:lo + 8]), F.Copy), [al("pb%d" % h)], [al("phw"), (on, lo, lo + 8)])
+
+    def p_turn(h):
+        vop(lambda: V.transpose(T["pt%d" % h][:], T["pb%d" % h][:]), [al("pt%d" % h)], [al("pb%d" % h)])
+
+    def turned(h, name, mat, last):
+        ps = "ps%d" % h
+        for u in range(2):
+            for w in range(2):
+                op("P", mm(T[ps][:, 64 * u:64 * u + 64], T[mat][:, 2 * u + w], T[name][:, :, 16 * w:16 * w + 16], False, last and u == 1 and w == 1),
+                   [al(ps)], [al(mat), al(name)])
+
+    def names(t, h):
+        (on, lo), nm = table(t, h), "nm%d" % h
+        vop(lambda: V.tensor_copy(T[nm][:], T.adjw[:, 0:3840].indirect(T[on][:, lo:lo + 8])), [al(nm)], [al("adjw"), (on, lo, lo + 8)])
+
+    def start(t, h, late_p=False):
+        nm, dr, aa, xr, ps, nf = ("%s%d" % (q, h) for q in ("nm", "dr", "aa", "xr", "ps", "nf"))
+        zz, z0, n0 = "zz%d" % (t // 4), 2048 * h, 128 * h
+        na = 8 - NPOS[t][h]
+        m = (na + 1) // 2
+        halves = [(a, b) for a, b in ((0, m), (m, na)) if a < b]
+        for a, b in halves:
+            vop(lambda: V.tensor_tensor(T[dr][:, 256 * a:256 * b], T.xw[:, 0:3840].indirect(T[nm][:, 16 * a:16 * b]), T[zz][:, z0 + 256 * a:z0 + 256 * b], A.subtract),
+                [(dr, 256 * a, 256 * b)], [al("xw"), al(nm), al(zz)])
+        vop(lambda: V.tensor_scalar(T[nf][:], T[nm][:], 1920.0, None, A.subtract), [al(nf)], [al(nm)])
+        vop(lambda: V.transpose(T["nt%d" % h][:], T[nf][:]), [al("nt%d" % h)], [al(nf)])
+        if not late_p:
+            p_gather(t, h)
+
+        def s_abs(a, b, src, s0):
+            op("S", lambda: S.activation(T[aa][:, 16 * a:16 * b, :], T[src][:, s0:s0 + 256 * (b - a)], F.Abs), [(aa, 256 * a, 256 * b)], [(src, s0, s0 + 256 * (b - a))])
+        op("P", mm(T[ps][:, 0:128], T.onesh[:], T.kc[:], True, False), [al(ps)], [al("onesh"), al("kc")])
+        if t == 0:
+            op("P", mm(T[ps][:, 0:128], T.idn[:], T.nts[:, n0:n0 + 128], False, False), [al(ps)], [al("idn"), al("nts")])
+        else:
+            for y in range(2):
+                q = 2 * (t - 1) + y
+                op("P", mm(T[ps][:, 0:128], T.sh[:, q, :], T.nts[:, n0 + 16 * y:n0 + 16 * y + 128], False, False), [al(ps)], [("sh", q, q + 1), al("nts")])
+        fs = []
+        for a in range(na, 8, 2):
+            b = min(a + 2, 8)
+            fb = "fb%d" % (fbn[0] % 2)
+            fbn[0] += 1
+            x0, x1 = 256 * (a - na), 256 * (b - na)
+            op("S", lambda: S.activation(T[xr][:, x0:x1], T.xw[:, 0:3840].indirect(T[nm][:, 16 * a:16 * b]), F.Copy), [(xr, x0, x1)], [al("xw"), al(nm)])
+            op("P", mm(T[fb][:, 0:x1 - x0], T.idm[:], T[zz][:, z0 + 256 * a:z0 + 256 * b], True, False), [al(fb)], [al("idm"), al(zz)])
+            op("P", mm(T[fb][:, 0:x1 - x0], T.idn[:], T[xr][:, x0:x1], False, True), [al(fb)], [al("idn"), (xr, x0, x1)])
+            if fs:
+                s_abs(*fs[-1])
+            fs.append((a, b, fb, 0))
+        for a, b in halves[:1]:
+            s_abs(a, b, dr, 256 * a)
+        s_abs(*fs[-1])
+        for a, b in halves[1:]:
+            s_abs(a, b, dr, 256 * a)
+
+    def sums(t, h, late_p=False):
+        aa, ps = "aa%d" % h, "ps%d" % h
+        turned(h, "nt%d" % h, "ef", False)
+        if not late_p:
+            p_turn(h)
+            turned(h, "pt%d" % h, "eb", False)
+        for r in range(16):
+            for u in range(2):
+                op("P", mm(T[ps][:, 64 * u:64 * u + 64], T.bsl[:, 15 - r:143 - r], T[aa][:, 16 * u + r::32, :], False, (not late_p) and r == 15 and u == 1),
+                   [al(ps)], [al("bsl"), al(aa)])
+
+    def finish(t, h):
+        hi, sc, ni, ps = "hi%d" % (t // 4), "sc%d" % h, "ni%d" % h, "ps%d" % h
+        c0, o = 16 * (t % 4) + 8 * h, 16 * (t + 1) + 8 * h
+        vop(lambda: V.tensor_tensor_scan(T[sc][:], T.rst[:], T[ps][:, 0:128], 0.0, A.add, A.max), [al(sc)], [al("rst"), al(ps)])
+        vop(lambda: V.tensor_copy(T[hi][:, c0:c0 + 8], T[sc][:, 15:128:16]), [(hi, c0, c0 + 8)], [al(sc)])
+        vop(lambda: V.tensor_scalar(T[ni][:], T[hi][:, c0:c0 + 8], 4095, None, A.bitwise_and), [al(ni)], [(hi, c0, c0 + 8)])
+        for u in range(2):
+            vop(lambda: V.tensor_copy(T.off[:, o + u:o + 8:2], T[ni][:, 4 * u:4 * u + 4]), [("off", o + 4 * u, o + 4 * u + 4)], [al(ni)])
+        if t in (3, 7):
+            i = t // 4 + 1
+            send(nxt, T["offi%d" % i][:, 8 * h:8 * h + 8], T.off[:, o:o + 8], "o%d%d" % (i, h), ("off", o, o + 8), ("offi%d" % i, 8 * h, 8 * h + 8))
+
+    def distance(i):
+        o, zz, ds = 64 * (i + 1), "zz%d" % i, "ds%d" % i
+        vop(lambda: V.tensor_tensor(T.dg[:], T.xw[:, 0:3840].indirect(T.off[:, o:o + 16]), T[zz][:, 0::16], A.subtract), [al("dg")], [al("xw"), ("off", o, o + 16), al(zz)])
+        op("S", lambda: S.activation(T.da[:], T.dg[:], F.Abs), [al("da")], [al("dg")])
+        for r in range(16):
+            op("P", mm(T.pm[:, 0:16], T.bsl[:, 15 - r:143 - r], T.da[:, :, r], r == 0, r == 15), [al("pm")], [al("bsl"), al("da")])
+        op("S", lambda: S.activation(T[ds][:], T.pm[:, 0:16], F.Copy), [al(ds)], [al("pm")])
+        if i > 0:
+            send(prv, T["din%d" % i][:], T[ds][:], "d%d" % i, al(ds), al("din%d" % i))
+
+    def trail(v):
+        L = []
+        hi, nv, uf, ud, ul, kl, dl, ubc, eq = ("%s%d" % (q, v) for q in ("hi", "nv", "uf", "ud", "ul", "kl", "dl", "ubc", "eq"))
+
+        def c(f, w, r):
+            L.append(lambda: vop(f, w, r))
+
+        def tt(out, a, b, o, w, r):
+            c(lambda: V.tensor_tensor(out, a, b, o), w, r)
+
+        def ts(out, a, s1, s2, o1, o2, w, r):
+            c(lambda: V.tensor_scalar(out, a, s1, None, o1) if s2 is None else V.tensor_scalar(out, a, s1, s2, o1, o2), w, r)
+        if v == 0:
+            c(lambda: V.tensor_copy(T[nv][:, 0:16], T.v0t[:]), [(nv, 0, 16)], [al("v0t")])
+        else:
+            for h, u in HU:
+                a = 8 * h + 4 * u
+                c(lambda h=h, u=u, a=a: V.tensor_copy(T[nv][:, a:a + 4], T["offi%d" % v][:, 8 * h + u:8 * h + 8:2]), [(nv, a, a + 4)], [("offi%d" % v, 8 * h, 8 * h + 8)])
+        ts(T[nv][:, 16:80], T[hi][:], 4095, None, A.bitwise_and, None, [(nv, 16, 80)], [al(hi)])
+        ts(T.kv[:], T[hi][:], 12, 15, A.arith_shift_right, A.bitwise_and, [al("kv")], [al(hi)])
+        c(lambda: V.memset(T.al[:], 1.0), [al("al")], [])
+        for d in range(1, 5):
+            tt(T.ee[:, d - 1:4, 16 * (5 - d):16 * (6 - d)], T[nv][:, 0:16 * (5 - d)], T[nv][:, 16 * d:80], A.is_equal, [("ee", d, d + 1)], [al(nv)])
+        ts(T.cod[:], T.kv[:], 4096.0, 65536.0, A.mult, A.add, [al("cod")], [al("kv")])
+        tt(T.cod[:], T.cod[:], T[nv][:, 0:64], A.add, [al("cod")], [al("cod"), al(nv)])
+        for s in range(1, 5):
+            e0, n = 16 * (5 - s), 16 * (s - 1)
+            if s == 1:
+                c(lambda: V.tensor_copy(T.hh[:, 0:16], T.ee[:, 0, 64:80]), [("hh", 0, 16)], [al("ee")])
+            else:
+                tt(T.hh[:, 0:n], T.al[:, 0:n], T.ee[:, s - 1, e0:e0 + n], A.mult, [("hh", 0, n)], [al("al"), al("ee")])
+                for q in range(16, n, 16):
+                    tt(T.hh[:, q:q + 16], T.hh[:, q - 16:q], T.hh[:, q:q + 16], A.add, [("hh", q, q + 16)], [("hh", q - 16, q + 16)])
+                tt(T.hh[:, n:n + 16], T.hh[:, n - 16:n], T.ee[:, s - 1, 64:80], A.add, [("hh", n, n + 16)], [("hh", n - 16, n), al("ee")])
+            tt(T.al[:, 0:16 * s], T.al[:, 0:16 * s], T.hh[:, 0:16 * s], A.is_gt, [("al", 0, 16 * s)], [al("al"), ("hh", 0, 16 * s)])
+        c(lambda: V.memset(T.pl[:, 0:16], 0.0), [("pl", 0, 16)], [])
+        for q in (16, 32, 48):
+            tt(T.pl[:, q:q + 16], T.pl[:, q - 16:q], T.al[:, q - 16:q], A.add, [("pl", q, q + 16)], [("pl", q - 16, q), al("al")])
+        ts(T.na[:], T.al[:], -9.0, 9.0, A.mult, A.add, [al("na")], [al("al")])
+        tt(T.pl[:], T.pl[:], T.na[:], A.add, [al("pl")], [al("pl"), al("na")])
+        for p in range(4):
+            ts(T.ww[:, p, :], T.pl[:], float(p), None, A.is_equal, None, [("ww", p, p + 1)], [al("pl")])
+        for p in range(4):
+            tt(T.w2[:, p], T.ww[:, p, :], T.cod[:], A.mult, [("w2", p, p + 1)], [("ww", p, p + 1), al("cod")])
+        tt(T.w3[:], T.w2[:, :, 0:2, :], T.w2[:, :, 2:4, :], A.add, [al("w3")], [al("w2")])
+        tt(T.cp[:], T.w3[:, :, 0, :], T.w3[:, :, 1, :], A.add, [al("cp")], [al("w3")])
+        c(lambda: V.tensor_copy(T.ci[:], T.cp[:]), [al("ci")], [al("cp")])
+        ts(T.nx[:], T.cp[:], 0.0, None, A.is_equal, None, [al("nx")], [al("cp")])
+        tt(T.nx[:], T.nx[:], T.dum[:], A.mult, [al("nx")], [al("nx"), al("dum")])
+        ts(T.kv[:], T.ci[:], 12, 15, A.arith_shift_right, A.bitwise_and, [al("kv")], [al("ci")])
+        ts(T.ci[:], T.ci[:], 4095, None, A.bitwise_and, None, [al("ci")], [al("ci")])
+        tt(T[uf][:], T.ci[:], T.nx[:], A.add, [al(uf)], [al("ci"), al("nx")])
+        c(lambda: V.tensor_copy(T[ul][:], T[uf][:]), [al(ul)], [al(uf)])
+        tt(T[ud][:], T[uf][:], T.dum[:], A.subtract, [al(ud)], [al(uf), al("dum")])
+        ts(T[kl][:], T.kv[:], -1.0, 15.0, A.mult, A.add, [al(kl)], [al("kv")])
+        for p in range(4):
+            L.append(lambda p=p: op("S", lambda: S.activation(T[dl][:, 256 * p:256 * p + 256], T.dwin[:, 0:16].indirect(T[kl][:, 16 * p:16 * p + 16]), F.Copy),
+                                    [(dl, 256 * p, 256 * p + 256)], [al("dwin"), al(kl)]))
+            c(lambda p=p: V.tensor_copy(T[ubc][:, 256 * p:256 * p + 256], T.iw[:, 0:4096].indirect(T[ul][:, 16 * p:16 * p + 16])), [(ubc, 256 * p, 256 * p + 256)], [al("iw"), al(ul)])
+            for q in range(16 * p, 16 * p + 16):
+                j, a = q % 8, 128 * (q // 8)
+                ts(T[eq][:, q, 0:128 - 16 * j], T[ubc][:, a + 16 * j:a + 128], T[uf][:, q:q + 1], None, A.is_equal, None, [(eq, 128 * q, 128 * q + 128)], [(ubc, a, a + 128), al(uf)])
+        for x in range(16):
+            L.append(lambda x=x: op("S", lambda: S.activation(T[eq][:, :, x], T[eq][:, :, x], F.Copy, scale=T.mw[:, x:x + 1]), [al(eq)], [al(eq), al("mw")]))
+        return L
+
+    def better(v, third):
+        eq, din, ds = "eq%d" % v, "din%d" % (v + 1), "ds%d" % v
+        vop(lambda: V.tensor_tensor(T.bet[:], T[din][:], T[ds][:], A.is_gt), [al("bet")], [al(din), al(ds)])
+        for c in range(16):
+            pos = 8 * (c // 8) + 2 * (c % 4) + (c % 8) // 4
+            if c % 3 != third:
+                vop(lambda: V.tensor_scalar(T.bt[:, c, :], T.bm[:], T.bet[:, pos:pos + 1], None, A.mult), [("bt", c, c + 1)], [al("bm"), al("bet")])
+            else:
+                op("S", lambda: S.activation(T.bt[:, c, :], T.bm[:], F.Copy, scale=T.bet[:, pos:pos + 1]), [("bt", c, c + 1)], [al("bm"), al("bet")])
+        for p in range(4):
+            cn, base = BANK[p]
+            if base == 0:
+                n = 2 if p == 1 else 1
+                op("P", mm(T[cn][:, 0:256 * n], T.idn[:], T.pen[:, 0:16 * n, :], True, False), [al(cn)], [al("idn"), al("pen")])
+            for c in range(16):
+                j, q, o = c % 8, 16 * p + c, base + 128 * (c // 8)
+                op("P", mm(T[cn][:, o + 16 * j:o + 128], T.bt[:, c, :], T[eq][:, q, 0:128 - 16 * j], False, c == 15 and p != 1),
+                   [al(cn)], [("bt", c, c + 1), (eq, 128 * q, 128 * q + 128)])
+
+    def chain(v, fill):
+        ud, dl = "ud%d" % v, "dl%d" % v
+        for p in range(4):
+            if p < 2:
+                o, n = (0, 16) if p == 0 else (16, 48)
+                for cn, s0, w in ([("cn0", 0, 256)] if p == 0 else [("cn1", 0, 512), ("cn2", 512, 256)]):
+                    vop(lambda: V.tensor_tensor_scan(T.scn[:, s0:s0 + w], T.rsp[:, 0:w], T[cn][:, 0:w], 1.0e6, A.add, A.min), [("scn", s0, s0 + w)], [al("rsp"), al(cn)])
+                vop(lambda: V.tensor_scalar(T.okm[:, 0:n], T.scn[:, 15:16 * n:16], 0.5, None, A.is_equal), [al("okm")], [al("scn")])
+                vop(lambda: V.tensor_tensor(T.okm[:, 0:n], T.okm[:, 0:n], T[ud][:, o:o + n], A.mult), [al("okm")], [al("okm"), al(ud)])
+                vop(lambda: V.tensor_tensor(T.okm[:, 0:n], T.okm[:, 0:n], T.dum[:, o:o + n], A.add), [al("okm")], [al("okm"), al("dum")])
+                vop(lambda: V.tensor_copy(T.ofl[:, o:o + n], T.okm[:, 0:n]), [("ofl", o, o + n)], [al("okm")])
+            vop(lambda: V.tensor_tensor(T.t1[:], T.phw[:, 0:4096].indirect(T.ofl[:, 16 * p:16 * p + 16]), T[dl][:, 256 * p:256 * p + 256], A.add),
+                [al("t1")], [al("phw"), ("ofl", 16 * p, 16 * p + 16), (dl, 256 * p, 256 * p + 256)])
+            fill(FG)
+            vop(lambda: V.tensor_scalar(T.t2[:], T.t1[:], 0.0, 20.0, A.max, A.min), [al("t2")], [al("t1")])
+            fill(FG)
+            for h in (1, 0):
+                vop(lambda: V.tensor_copy(T.phw[:, 0:4096].indirect(T.ofl[:, 16 * p + 8 * h:16 * p + 8 * h + 8]), T.t2[:, 128 * h:128 * h + 128]),
+                    [al("phw")], [al("t2"), ("ofl", 16 * p, 16 * p + 16)])
+                fill(FG)
+
+    queue = late_constants()
+
+    def fill(n):
+        for _ in range(min(n, len(queue))):
+            queue.pop(0)()
+
+    for t in range(12):
+        if t in (4, 8):
+            v = t // 4 - 1
+            finish(t - 1, 0)
+            fill(KEEP[v])
+            finish(t - 1, 1)
+            if v == 1:
+                distance(1)
+            fill(len(queue))
+            queue.extend(trail(v))
+            if v == 0:
+                fill(FB[0])
+                queue.insert(20, lambda: distance(0))
+            else:
+                fill(FB[1])
+        if t == 8:
+            names(8, 0)
+            start(8, 0, True)
+            names(8, 1)
+            fill(FR[0])
+            better(0, 9)
+            sums(8, 0, True)
+            start(8, 1, True)
+            sums(8, 1, True)
+            fill(FR[1])
+            chain(0, fill)
+            for h in range(2):
+                p_gather(8, h)
+                p_turn(h)
+                turned(h, "pt%d" % h, "eb", True)
+            continue
+        for h in range(2):
+            if t % 4:
+                finish(t - 1, h)
+            names(t, h)
+            start(t, h)
+            sums(t, h)
+            if t > 3:
+                left = 2 * (4 - t % 4) - h
+                fill(max(0, -(-(len(queue) - (KEEP[1] if t < 8 else 0)) // left)))
+    fill(len(queue))
+    finish(11, 0)
+    finish(11, 1)
+    distance(2)
+    vop(lambda: V.tensor_scalar(T.yvi[:], T.hi2[:, 48:64], 4095, None, A.bitwise_and), [al("yvi")], [("hi2", 48, 64)])
+    vop(lambda: V.tensor_copy(T.yvt[:], T.yvi[:]), [al("yvt")], [al("yvi")])
+    op("Y", lambda: g.sync.dma_start(T.yv[:], T.yvt[:]), [], [al("yvt")], "ov", 16)
+    better(1, 2)
+    chain(1, fill)
+    op("Y", lambda: g.sync.dma_start(T.yp[:, 0:1920], T.phw[:, 0:1920]), [], [("phw", 0, 1920)], "oy0", 16)
+    op("S", lambda: g.scalar.dma_start(T.yp[:, 1920:3840], T.phw[:, 1920:3840]), [], [("phw", 1920, 3840)], "oy1", 16)
+    for s, v in cnt.items():
+        need("G", (s, v))

@@ -1,7 +1,7 @@
 from concourse.mybir import AluOpType as A, ActivationFunctionType as F
 
-NPOS = [(2, 2)] * 4 + [(3, 3)] * 4 + [(8, 8)] + [(4, 4)] * 3
-FR, FG, FB, KEEP = (20, 8), 1, (12, 0), (30, 22)
+NPOS = [(3, 2)] * 4 + [(3, 4)] * 4 + [(8, 8)] + [(3, 4)] * 2 + [(3, 2)]
+FR, KEEP = (20, 8), 50
 BANK = [("cn0", 0), ("cn1", 0), ("cn1", 256), ("cn2", 0)]
 CLAIM = 65536.0
 BF, FH, F4, I4, U2 = "bfloat16", "float16", "float32", "int32", "uint16"
@@ -36,8 +36,16 @@ def rank_program(g, core, T, topo):
     ENG = {"V": g.vector, "S": g.scalar, "P": g.tensor, "G": g, "Y": g.sync}
     OWN = {"V": "sv", "S": "ss", "P": "sp", "G": "sg"}
     V, S, P = g.vector, g.scalar, g.tensor
-    cnt, snap, writes, reads = {}, {}, {}, {}
+    cnt, snap, writes, reads = {"sv": 0}, {}, {}, {}
     clk = {e: {} for e in ENG}
+    soft, queue, pending, busy = [], [], [], []
+
+    def fill(n):
+        busy.append(1)
+        for _ in range(n):
+            if soft or queue:
+                (soft or queue).pop(0)()
+        busy.pop()
 
     def need(e, tok):
         sem, val = tok
@@ -68,6 +76,8 @@ def rank_program(g, core, T, topo):
                     for x in hits(reads, b, lo, hi):
                         if x[3] != e:
                             dep(x[2])
+        if e == "V" and not busy and deps.get("sv", 0) == cnt["sv"] > clk["V"].get("sv", 0):
+            fill(1)
         for tok in sorted(deps.items(), key=lambda t: -t[1]):
             need(e, tok)
         ins = make()
@@ -111,6 +121,9 @@ def rank_program(g, core, T, topo):
         op("G", lambda: g.affine_select(T.ef[:, i, :, w, :], T.onesh[:, 0:64], [[32, 4], [1, 16]], A.is_equal, 0.0, 16 * u, -1),
            [("ef", 128 * i, 128 * i + 128)], [al("onesh")])
     op("G", lambda: g.affine_select(T.idn[:], T.ones[:], [[16, 8], [1, 16]], A.is_equal, 0.0, 0, -1), [al("idn")], [al("ones")])
+    op("G", lambda: g.iota(T.rri[:], [[0, 2]], 0, 1), [al("rri")], [])
+    op("G", lambda: g.iota(T.dum[:], [[0, 4], [16, 16]], 3840, 0, allow_small_or_imprecise_dtypes=True), [al("dum")], [])
+    op("G", lambda: g.iota(T.rowi[:], [[1, 16]], 0, 0, allow_small_or_imprecise_dtypes=True), [al("rowi")], [])
     for h, u in HU:
         vop(lambda: V.tensor_copy(T.zp[:, 4 * h:4 * h + 4, u, :], T.zt[:, 128 * h + 64 * u:128 * h + 64 * u + 64]), [("zp", 2 * h + u, 2 * h + u + 1)], [al("zt")])
     for k in range(16):
@@ -124,6 +137,19 @@ def rank_program(g, core, T, topo):
     vop(lambda: V.tensor_scalar(T.eb[:], T.ef[:], CLAIM, None, A.mult), [al("eb")], [al("ef")])
     vop(lambda: V.tensor_scalar(T.idm[:], T.idn[:], -1.0, None, A.mult), [al("idm")], [al("idn")])
     vop(lambda: V.memset(T.phw[:], 8.0), [al("phw")], [])
+    vop(lambda: V.tensor_scalar(T.rri[:], T.rri[:], 15, None, A.bitwise_and), [al("rri")], [al("rri")])
+    vop(lambda: V.tensor_copy(T.rrf[:], T.rri[:]), [al("rrf")], [al("rri")])
+    vop(lambda: V.tensor_scalar(T.dum[:], T.dum[:], T.rrf[:, 0:1], None, A.add), [al("dum")], [al("dum"), al("rrf")])
+    vop(lambda: V.tensor_scalar(T.dwin[:], T.rowi[:], T.rrf[:, 0:1], None, A.is_equal), [al("dwin")], [al("rowi"), al("rrf")])
+    vop(lambda: V.tensor_scalar(T.mw[:], T.rowi[:], T.rrf[:, 0:1], None, A.is_gt), [al("mw")], [al("rowi"), al("rrf")])
+    vop(lambda: V.tensor_scalar(T.dlt[:], T.dwin[:], 0.5, None, A.mult), [al("dlt")], [al("dwin")])
+    vop(lambda: V.tensor_tensor(T.mw[:], T.mw[:], T.dlt[:], A.add), [al("mw")], [al("mw"), al("dlt")])
+    vop(lambda: V.tensor_scalar(T.pen[:, 0, :], T.dwin[:], -1024.0, 1024.0, A.mult, A.add), [("pen", 0, 1)], [al("dwin")])
+    vop(lambda: V.tensor_scalar(T.dwin[:], T.dwin[:], 11.0, -3.0, A.mult, A.add), [al("dwin")], [al("dwin")])
+    for n in (1, 2, 4, 8, 16):
+        vop(lambda: V.tensor_copy(T.pen[:, n:2 * n, :], T.pen[:, 0:n, :]), [("pen", n, 2 * n)], [("pen", 0, n)])
+    vop(lambda: V.memset(T.rsp[:], 0.0), [al("rsp")], [])
+    vop(lambda: V.memset(T.rsp[:, 0::16], 1.0e6), [al("rsp")], [])
     for h, u in HU:
         vop(lambda: V.tensor_copy(T.off[:, 8 * h + u:8 * h + 8:2], T.v0t[:, 8 * h + 4 * u:8 * h + 4 * u + 4]), [("off", 8 * h + 4 * u, 8 * h + 4 * u + 4)], [al("v0t")])
     for h, u in HU:
@@ -155,29 +181,6 @@ def rank_program(g, core, T, topo):
         if t == 4:
             send(nx2, T.zz2[:], T.zz0[:], "z2", al("zz0"), al("zz2"))
             op("G", lambda: g.iota(T.iw[:], [[1, 4096]], 0, 0), [al("iw")], [])
-            op("G", lambda: g.iota(T.rri[:], [[0, 2]], 0, 1), [al("rri")], [])
-            op("G", lambda: g.iota(T.dum[:], [[0, 4], [16, 16]], 3840, 0, allow_small_or_imprecise_dtypes=True), [al("dum")], [])
-            op("G", lambda: g.iota(T.rowi[:], [[1, 16]], 0, 0, allow_small_or_imprecise_dtypes=True), [al("rowi")], [])
-
-    def late_constants():
-        L = []
-
-        def c(f, w, r):
-            L.append(lambda: vop(f, w, r))
-        c(lambda: V.tensor_scalar(T.rri[:], T.rri[:], 15, None, A.bitwise_and), [al("rri")], [al("rri")])
-        c(lambda: V.tensor_copy(T.rrf[:], T.rri[:]), [al("rrf")], [al("rri")])
-        c(lambda: V.tensor_scalar(T.dum[:], T.dum[:], T.rrf[:, 0:1], None, A.add), [al("dum")], [al("dum"), al("rrf")])
-        c(lambda: V.tensor_scalar(T.dwin[:], T.rowi[:], T.rrf[:, 0:1], None, A.is_equal), [al("dwin")], [al("rowi"), al("rrf")])
-        c(lambda: V.tensor_scalar(T.mw[:], T.rowi[:], T.rrf[:, 0:1], None, A.is_gt), [al("mw")], [al("rowi"), al("rrf")])
-        c(lambda: V.tensor_scalar(T.dlt[:], T.dwin[:], 0.5, None, A.mult), [al("dlt")], [al("dwin")])
-        c(lambda: V.tensor_tensor(T.mw[:], T.mw[:], T.dlt[:], A.add), [al("mw")], [al("mw"), al("dlt")])
-        c(lambda: V.tensor_scalar(T.pen[:, 0, :], T.dwin[:], -1024.0, 1024.0, A.mult, A.add), [("pen", 0, 1)], [al("dwin")])
-        c(lambda: V.tensor_scalar(T.dwin[:], T.dwin[:], 11.0, -3.0, A.mult, A.add), [al("dwin")], [al("dwin")])
-        for n in (1, 2, 4, 8, 16):
-            c(lambda n=n: V.tensor_copy(T.pen[:, n:2 * n, :], T.pen[:, 0:n, :]), [("pen", n, 2 * n)], [("pen", 0, n)])
-        c(lambda: V.memset(T.rsp[:], 0.0), [al("rsp")], [])
-        c(lambda: V.memset(T.rsp[:, 0::16], 1.0e6), [al("rsp")], [])
-        return L
 
     fbn = [0]
 
@@ -203,7 +206,7 @@ def rank_program(g, core, T, topo):
         vop(lambda: V.tensor_copy(T[nm][:], T.adjw[:, 0:3840].indirect(T[on][:, lo:lo + 8])), [al(nm)], [al("adjw"), (on, lo, lo + 8)])
 
     def start(t, h, late_p=False):
-        nm, dr, aa, xr, ps, nf = ("%s%d" % (q, h) for q in ("nm", "dr", "aa", "xr", "ps", "nf"))
+        nm, dr, aa, xr, ps, nf, nt = ("%s%d" % (q, h) for q in ("nm", "dr", "aa", "xr", "ps", "nf", "nt"))
         zz, z0, n0 = "zz%d" % (t // 4), 2048 * h, 128 * h
         na = 8 - NPOS[t][h]
         m = (na + 1) // 2
@@ -211,10 +214,11 @@ def rank_program(g, core, T, topo):
         for a, b in halves:
             vop(lambda: V.tensor_tensor(T[dr][:, 256 * a:256 * b], T.xw[:, 0:3840].indirect(T[nm][:, 16 * a:16 * b]), T[zz][:, z0 + 256 * a:z0 + 256 * b], A.subtract),
                 [(dr, 256 * a, 256 * b)], [al("xw"), al(nm), al(zz)])
-        vop(lambda: V.tensor_scalar(T[nf][:], T[nm][:], 1920.0, None, A.subtract), [al(nf)], [al(nm)])
-        vop(lambda: V.transpose(T["nt%d" % h][:], T[nf][:]), [al("nt%d" % h)], [al(nf)])
+        soft.append(lambda: vop(lambda: V.tensor_scalar(T[nf][:], T[nm][:], 1920.0, None, A.subtract), [al(nf)], [al(nm)]))
+        soft.append(lambda: vop(lambda: V.transpose(T[nt][:], T[nf][:]), [al(nt)], [al(nf)]))
         if not late_p:
             p_gather(t, h)
+            soft.append(lambda: p_turn(h))
 
         def s_abs(a, b, src, s0):
             op("S", lambda: S.activation(T[aa][:, 16 * a:16 * b, :], T[src][:, s0:s0 + 256 * (b - a)], F.Abs), [(aa, 256 * a, 256 * b)], [(src, s0, s0 + 256 * (b - a))])
@@ -234,25 +238,29 @@ def rank_program(g, core, T, topo):
             op("S", lambda: S.activation(T[xr][:, x0:x1], T.xw[:, 0:3840].indirect(T[nm][:, 16 * a:16 * b]), F.Copy), [(xr, x0, x1)], [al("xw"), al(nm)])
             op("P", mm(T[fb][:, 0:x1 - x0], T.idm[:], T[zz][:, z0 + 256 * a:z0 + 256 * b], True, False), [al(fb)], [al("idm"), al(zz)])
             op("P", mm(T[fb][:, 0:x1 - x0], T.idn[:], T[xr][:, x0:x1], False, True), [al(fb)], [al("idn"), (xr, x0, x1)])
-            if fs:
-                s_abs(*fs[-1])
             fs.append((a, b, fb, 0))
-        for a, b in halves[:1]:
+            if len(fs) > 1 and b < 8:
+                s_abs(*fs.pop(0))
+        for a, b in halves:
             s_abs(a, b, dr, 256 * a)
-        s_abs(*fs[-1])
-        for a, b in halves[1:]:
-            s_abs(a, b, dr, 256 * a)
+        for q in fs:
+            s_abs(*q)
 
     def sums(t, h, late_p=False):
         aa, ps = "aa%d" % h, "ps%d" % h
         turned(h, "nt%d" % h, "ef", False)
         if not late_p:
-            p_turn(h)
             turned(h, "pt%d" % h, "eb", False)
         for r in range(16):
             for u in range(2):
                 op("P", mm(T[ps][:, 64 * u:64 * u + 64], T.bsl[:, 15 - r:143 - r], T[aa][:, 16 * u + r::32, :], False, (not late_p) and r == 15 and u == 1),
                    [al(ps)], [al("bsl"), al(aa)])
+
+    def settle():
+        while soft:
+            fill(1)
+        while pending:
+            sums(*pending.pop(0))
 
     def finish(t, h):
         hi, sc, ni, ps = "hi%d" % (t // 4), "sc%d" % h, "ni%d" % h, "ps%d" % h
@@ -361,7 +369,7 @@ def rank_program(g, core, T, topo):
                 op("P", mm(T[cn][:, o + 16 * j:o + 128], T.bt[:, c, :], T[eq][:, q, 0:128 - 16 * j], False, c == 15 and p != 1),
                    [al(cn)], [("bt", c, c + 1), (eq, 128 * q, 128 * q + 128)])
 
-    def chain(v, fill):
+    def chain(v):
         ud, dl = "ud%d" % v, "dl%d" % v
         for p in range(4):
             if p < 2:
@@ -374,70 +382,67 @@ def rank_program(g, core, T, topo):
                 vop(lambda: V.tensor_copy(T.ofl[:, o:o + n], T.okm[:, 0:n]), [("ofl", o, o + n)], [al("okm")])
             vop(lambda: V.tensor_tensor(T.t1[:], T.phw[:, 0:4096].indirect(T.ofl[:, 16 * p:16 * p + 16]), T[dl][:, 256 * p:256 * p + 256], A.add),
                 [al("t1")], [al("phw"), ("ofl", 16 * p, 16 * p + 16), (dl, 256 * p, 256 * p + 256)])
-            fill(FG)
             vop(lambda: V.tensor_scalar(T.t2[:], T.t1[:], 0.0, 20.0, A.max, A.min), [al("t2")], [al("t1")])
-            fill(FG)
             for h in (1, 0):
                 vop(lambda: V.tensor_copy(T.phw[:, 0:4096].indirect(T.ofl[:, 16 * p + 8 * h:16 * p + 8 * h + 8]), T.t2[:, 128 * h:128 * h + 128]),
                     [al("phw")], [al("t2"), ("ofl", 16 * p, 16 * p + 16)])
-                fill(FG)
-
-    queue = late_constants()
-
-    def fill(n):
-        for _ in range(min(n, len(queue))):
-            queue.pop(0)()
 
     for t in range(12):
         if t in (4, 8):
             v = t // 4 - 1
             finish(t - 1, 0)
-            fill(KEEP[v])
+            settle()
+            fill(KEEP)
             finish(t - 1, 1)
             if v == 1:
                 distance(1)
             fill(len(queue))
             queue.extend(trail(v))
             if v == 0:
-                fill(FB[0])
                 queue.insert(20, lambda: distance(0))
-            else:
-                fill(FB[1])
         if t == 8:
             names(8, 0)
             start(8, 0, True)
             names(8, 1)
             fill(FR[0])
             better(0, 9)
+            while soft:
+                fill(1)
             sums(8, 0, True)
             start(8, 1, True)
+            while soft:
+                fill(1)
             sums(8, 1, True)
             fill(FR[1])
-            chain(0, fill)
+            chain(0)
             for h in range(2):
                 p_gather(8, h)
                 p_turn(h)
                 turned(h, "pt%d" % h, "eb", True)
             continue
         for h in range(2):
+            n = len(queue)
             if t % 4:
                 finish(t - 1, h)
             names(t, h)
+            settle()
             start(t, h)
-            sums(t, h)
+            pending.append((t, h))
             if t > 3:
                 left = 2 * (4 - t % 4) - h
-                fill(max(0, -(-(len(queue) - (KEEP[1] if t < 8 else 0)) // left)))
-    fill(len(queue))
+                fill(max(0, -(-(n - (KEEP if t < 8 else 0)) // left) - n + len(queue) + len(soft)))
+    fill(len(queue) + len(soft))
     finish(11, 0)
+    settle()
     finish(11, 1)
     distance(2)
     vop(lambda: V.tensor_scalar(T.yvi[:], T.hi2[:, 48:64], 4095, None, A.bitwise_and), [al("yvi")], [("hi2", 48, 64)])
     vop(lambda: V.tensor_copy(T.yvt[:], T.yvi[:]), [al("yvt")], [al("yvi")])
     op("Y", lambda: g.sync.dma_start(T.yv[:], T.yvt[:]), [], [al("yvt")], "ov", 16)
     better(1, 2)
-    chain(1, fill)
+    chain(1)
     op("Y", lambda: g.sync.dma_start(T.yp[:, 0:1920], T.phw[:, 0:1920]), [], [("phw", 0, 1920)], "oy0", 16)
     op("S", lambda: g.scalar.dma_start(T.yp[:, 1920:3840], T.phw[:, 1920:3840]), [], [("phw", 1920, 3840)], "oy1", 16)
     for s, v in cnt.items():
-        need("G", (s, v))
+        if v:
+            need("G", (s, v))

from concourse.mybir import AluOpType as A, ActivationFunctionType as F

NPOS = [(3, 2)] * 4 + [(3, 4)] * 4 + [(8, 8)] + [(3, 4)] * 2 + [(3, 2)]
FR, KEEP = (20, 8), 50
BANK = [("cn0", 0), ("cn1", 0), ("cn1", 256), ("cn2", 0)]
CLAIM = 65536.0
BF, FH, F4, I4, U2 = "bfloat16", "float16", "float32", "int32", "uint16"
SCRATCH = {n: ("sbuf", [128] + s, d) for n, s, d in [
    ("adjw", [3840], I4), ("xw", [3840], BF), ("phw", [4096], BF), ("v0t", [16], I4), ("zt", [256], BF), ("nzt", [256], BF),
    ("zp", [8, 2, 16], BF), ("nzp", [8, 2, 16], BF), ("nzq", [8, 32], BF), ("nts", [272], BF),
    ("zz0", [4096], BF), ("zz1", [4096], BF), ("zz2", [4096], BF), ("off", [208], U2), ("offi1", [16], U2), ("offi2", [16], U2),
    ("ones", [8, 16], BF), ("bm", [8, 16], BF), ("idn", [8, 16], BF), ("idm", [128], BF), ("onesh", [128], FH), ("kcf", [128], F4),
    ("kc", [128], FH), ("bsl", [144], BF), ("ef", [4, 4, 2, 16], FH), ("eb", [4, 128], BF), ("sh", [22, 128], BF),
    ("rst", [128], F4), ("rsp", [512], F4), ("iw", [4096], I4), ("rri", [2], I4), ("rrf", [2], F4), ("dum", [64], F4),
    ("dlt", [16], F4), ("pen", [32, 16], BF), ("dwin", [16], BF), ("mw", [16], F4), ("rowi", [16], F4), ("dg", [256], BF),
    ("da", [16, 16], BF), ("ds0", [16], F4), ("ds1", [16], F4), ("ds2", [16], F4), ("din1", [16], F4), ("din2", [16], F4),
    ("bet", [16], F4), ("bt", [16, 128], BF), ("ee", [4, 80], F4), ("al", [64], F4), ("hh", [64], F4), ("pl", [64], F4),
    ("na", [64], F4), ("cod", [64], F4), ("ww", [4, 64], F4), ("w2", [4, 4, 16], F4), ("w3", [4, 2, 16], F4), ("cp", [4, 16], F4),
    ("ci", [64], I4), ("nx", [64], F4), ("kv", [64], I4), ("scn", [768], F4), ("okm", [48], F4), ("ofl", [64], U2),
    ("t1", [256], BF), ("t2", [256], BF), ("yvt", [16], F4), ("yvi", [16], I4), ("hi2", [64], I4)]}
SCRATCH.update({n: ("psum", [128, 512], F4) for n in ("fb0", "fb1", "ps0", "ps1", "cn0", "cn1", "cn2", "pm")})
for _h in "01":
    SCRATCH.update({n + _h: ("sbuf", [128] + s, d) for n, s, d in [
        ("nm", [128], U2), ("nf", [128], FH), ("nt", [4, 32], FH), ("pb", [128], BF), ("pt", [4, 32], BF), ("dr", [2048], BF),
        ("aa", [128, 16], BF), ("xr", [2048], BF), ("sc", [128], F4), ("ni", [8], I4), ("hi", [64], I4), ("nv", [80], I4),
        ("uf", [64], F4), ("ud", [64], F4), ("ul", [64], U2), ("kl", [64], U2), ("dl", [1024], BF), ("ubc", [1024], U2),
        ("eq", [64, 128], BF)]})
SEMAPHORES = ["sv", "ss", "sp", "sg", "la0", "la1", "lx", "lz", "ln", "lv", "oy0", "oy1", "ov"]
SEMAPHORES += [a + b for a in "rt" for b in ("z1", "z2", "o10", "o11", "o20", "o21", "d1", "d2")]


def rank_program(g, core, T, topo):
    rank = T.rank_of(core)
    if rank is None:
        return
    ENG = {"V": g.vector, "S": g.scalar, "P": g.tensor, "G": g, "Y": g.sync}
    OWN = {"V": "sv", "S": "ss", "P": "sp", "G": "sg"}
    V, S, P = g.vector, g.scalar, g.tensor
    cnt, snap, writes, reads = {"sv": 0}, {}, {}, {}
    clk = {e: {} for e in ENG}
    soft, queue, pending, busy = [], [], [], []

    def fill(n):
        busy.append(1)
        for _ in range(n):
            if soft or queue:
                (soft or queue).pop(0)()
        busy.pop()

    def need(e, tok):
        sem, val = tok
        c = clk[e]
        if c.get(sem, 0) >= val:
            return
        ENG[e].wait_ge(T.sem[sem], val)
        c[sem] = val
        for k, v in snap.get(tok, {}).items():
            if c.get(k, 0) < v:
                c[k] = v

    def hits(d, b, lo, hi):
        return [x for x in d.get(b, []) if x[0] < hi and lo < x[1]]

    def op(e, make, w=(), r=(), sem=None, inc=1):
        deps = {}

        def dep(tok):
            if deps.get(tok[0], 0) < tok[1]:
                deps[tok[0]] = tok[1]
        for k, regs in enumerate((r, w)):
            for b, lo, hi in regs:
                for x in hits(writes, b, lo, hi):
                    if not (e == "P" and x[3] == "P"):
                        dep(x[2])
                if k or SCRATCH[b][0] == "psum":
                    for x in hits(reads, b, lo, hi):
                        if x[3] != e:
                            dep(x[2])
        if e == "V" and not busy and deps.get("sv", 0) == cnt["sv"] > clk["V"].get("sv", 0):
            fill(1)
        for tok in sorted(deps.items(), key=lambda t: -t[1]):
            need(e, tok)
        ins = make()
        s = sem or OWN[e]
        if ins is not None:
            ins.then_inc(T.sem[s], inc)
        cnt[s] = cnt.get(s, 0) + inc
        tok = (s, cnt[s])
        snap[tok] = dict(clk[e])
        who = e if sem is None else "dma"
        for b, lo, hi in w:
            writes[b] = [x for x in writes.get(b, []) if not (lo <= x[0] and x[1] <= hi)] + [(lo, hi, tok, who)]
            reads[b] = [x for x in reads.get(b, []) if not (lo <= x[0] and x[1] <= hi)]
        for b, lo, hi in r:
            reads[b] = [x for x in reads.get(b, []) if not (x[3] == who and lo <= x[0] and x[1] <= hi)] + [(lo, hi, tok, who)]

    def al(b):
        return (b, 0, 1 << 20)

    def vop(f, w, r):
        op("V", f, w, r)

    def mm(*a):
        return lambda: P.matmul(*a)

    HU = [(h, u) for h in range(2) for u in range(2)]
    op("Y", lambda: g.sync.dma_start(T.zt[:], T.z[:]), [al("zt")], [], "lz", 16)
    op("S", lambda: g.scalar.dma_start(T.v0t[:], T.v0[:]), [al("v0t")], [], "lv", 16)
    op("S", lambda: g.scalar.dma_start(T.nzt[:], T.nz[:]), [al("nzt")], [], "ln", 16)
    op("Y", lambda: g.sync.dma_start(T.adjw[:, 0:1920], T.adj[:, 0:1920]), [("adjw", 0, 1920)], [], "la0", 16)
    op("S", lambda: g.scalar.dma_start(T.adjw[:, 1920:3840], T.adj[:, 1920:3840]), [("adjw", 1920, 3840)], [], "la1", 16)
    op("Y", lambda: g.sync.dma_start(T.xw[:], T.x[:]), [al("xw")], [], "lx", 16)
    vop(lambda: V.memset(T.ones[:], 1.0), [al("ones")], [])
    vop(lambda: V.memset(T.ef[:], 0.0), [al("ef")], [])
    vop(lambda: V.memset(T.onesh[:], 1.0), [al("onesh")], [])
    op("G", lambda: g.affine_select(T.bm[:], T.ones[:], [[-16, 8], [0, 16]], A.is_ge, 0.0, 0, 1), [al("bm")], [al("ones")])
    op("G", lambda: g.affine_select(T.bm[:], T.bm[:], [[16, 8], [0, 16]], A.is_ge, 0.0, 15, -1), [al("bm")], [al("bm")])
    op("G", lambda: g.iota(T.kcf[:], [[0, 8], [-32, 16]], 495, 0, allow_small_or_imprecise_dtypes=True), [al("kcf")], [])
    for u, w in HU:
        i = 2 * u + w
        op("G", lambda: g.affine_select(T.ef[:, i, :, w, :], T.onesh[:, 0:64], [[32, 4], [1, 16]], A.is_equal, 0.0, 16 * u, -1),
           [("ef", 128 * i, 128 * i + 128)], [al("onesh")])
    op("G", lambda: g.affine_select(T.idn[:], T.ones[:], [[16, 8], [1, 16]], A.is_equal, 0.0, 0, -1), [al("idn")], [al("ones")])
    op("G", lambda: g.iota(T.rri[:], [[0, 2]], 0, 1), [al("rri")], [])
    op("G", lambda: g.iota(T.dum[:], [[0, 4], [16, 16]], 3840, 0, allow_small_or_imprecise_dtypes=True), [al("dum")], [])
    op("G", lambda: g.iota(T.rowi[:], [[1, 16]], 0, 0, allow_small_or_imprecise_dtypes=True), [al("rowi")], [])
    for h, u in HU:
        vop(lambda: V.tensor_copy(T.zp[:, 4 * h:4 * h + 4, u, :], T.zt[:, 128 * h + 64 * u:128 * h + 64 * u + 64]), [("zp", 2 * h + u, 2 * h + u + 1)], [al("zt")])
    for k in range(16):
        vop(lambda: V.tensor_copy(T.zz0[:, k::16], T.zp[:]), [("zz0", k, k + 1)], [al("zp")])
    writes["zz0"] = [(0, 1 << 20, ("sv", cnt["sv"]), "V")]
    vop(lambda: V.memset(T.rst[:], 0.0), [al("rst")], [])
    vop(lambda: V.memset(T.rst[:, 0::16], -1.0e9), [al("rst")], [])
    vop(lambda: V.memset(T.bsl[:], 0.0), [al("bsl")], [])
    vop(lambda: V.tensor_scalar(T.bsl[:, 15:128:16], T.bm[:, :, 0], -CLAIM, None, A.mult), [al("bsl")], [al("bm")])
    vop(lambda: V.tensor_copy(T.kc[:], T.kcf[:]), [al("kc")], [al("kcf")])
    vop(lambda: V.tensor_scalar(T.eb[:], T.ef[:], CLAIM, None, A.mult), [al("eb")], [al("ef")])
    vop(lambda: V.tensor_scalar(T.idm[:], T.idn[:], -1.0, None, A.mult), [al("idm")], [al("idn")])
    vop(lambda: V.memset(T.phw[:], 8.0), [al("phw")], [])
    vop(lambda: V.tensor_scalar(T.rri[:], T.rri[:], 15, None, A.bitwise_and), [al("rri")], [al("rri")])
    vop(lambda: V.tensor_copy(T.rrf[:], T.rri[:]), [al("rrf")], [al("rri")])
    vop(lambda: V.tensor_scalar(T.dum[:], T.dum[:], T.rrf[:, 0:1], None, A.add), [al("dum")], [al("dum"), al("rrf")])
    vop(lambda: V.tensor_scalar(T.dwin[:], T.rowi[:], T.rrf[:, 0:1], None, A.is_equal), [al("dwin")], [al("rowi"), al("rrf")])
    vop(lambda: V.tensor_scalar(T.mw[:], T.rowi[:], T.rrf[:, 0:1], None, A.is_gt), [al("mw")], [al("rowi"), al("rrf")])
    vop(lambda: V.tensor_scalar(T.dlt[:], T.dwin[:], 0.5, None, A.mult), [al("dlt")], [al("dwin")])
    vop(lambda: V.tensor_tensor(T.mw[:], T.mw[:], T.dlt[:], A.add), [al("mw")], [al("mw"), al("dlt")])
    vop(lambda: V.tensor_scalar(T.pen[:, 0, :], T.dwin[:], -1024.0, 1024.0, A.mult, A.add), [("pen", 0, 1)], [al("dwin")])
    vop(lambda: V.tensor_scalar(T.dwin[:], T.dwin[:], 11.0, -3.0, A.mult, A.add), [al("dwin")], [al("dwin")])
    for n in (1, 2, 4, 8, 16):
        vop(lambda: V.tensor_copy(T.pen[:, n:2 * n, :], T.pen[:, 0:n, :]), [("pen", n, 2 * n)], [("pen", 0, n)])
    vop(lambda: V.memset(T.rsp[:], 0.0), [al("rsp")], [])
    vop(lambda: V.memset(T.rsp[:, 0::16], 1.0e6), [al("rsp")], [])
    for h, u in HU:
        vop(lambda: V.tensor_copy(T.off[:, 8 * h + u:8 * h + 8:2], T.v0t[:, 8 * h + 4 * u:8 * h + 4 * u + 4]), [("off", 8 * h + 4 * u, 8 * h + 4 * u + 4)], [al("v0t")])
    for h, u in HU:
        op("S", lambda: S.activation(T.nzp[:, 4 * h:4 * h + 4, u, :], T.nzt[:, 128 * h + 64 * u:128 * h + 64 * u + 64], F.Copy), [("nzp", 2 * h + u, 2 * h + u + 1)], [al("nzt")])
    vop(lambda: V.transpose(T.nzq[:], T.nzp[:]), [al("nzq")], [al("nzp")])
    for h, u in HU:
        for w in range(2):
            op("P", mm(T.pm[:, 128 * h + 64 * u:128 * h + 64 * u + 64], T.eb[:, 2 * u + w, :], T.nzq[:, 4 * h:4 * h + 4, 16 * w:16 * w + 16], w == 0, w == 1),
               [al("pm")], [al("eb"), al("nzq")])
    op("S", lambda: S.activation(T.nts[:, 0:256], T.pm[:, 0:256], F.Copy), [("nts", 0, 256)], [al("pm")])
    op("S", lambda: S.activation(T.nts[:, 256:272], T.pm[:, 0:16], F.Copy), [("nts", 256, 272)], [al("pm")])

    def send(dst, out, src, name, srcreg, landreg):
        m, n = topo.mask(core, dst), len(topo.engines(core, dst))
        rid, pid, _ = topo.addr(dst)

        def make():
            g.remote_dma(out, src, T.sem["r" + name], T.sem["t" + name], pid, rid, m)
        op("G", make, [], [srcreg], "t" + name, n)
        cnt["r" + name] = n
        writes.setdefault(landreg[0], []).append((landreg[1], landreg[2], ("r" + name, n), "rem"))

    nxt, nx2, prv = (T.cores[(rank + d) % 4] for d in (1, 2, 3))
    send(nxt, T.zz1[:], T.zz0[:], "z1", al("zz0"), al("zz1"))
    for t in range(1, 12):
        for y in range(2):
            i = 2 * (t - 1) + y
            op("G", lambda: g.affine_select(T.sh[:, i, :], T.bm[:], [[-16, 8], [-1, 16]], A.is_equal, 0.0, 16 * y - t, 1), [("sh", i, i + 1)], [al("bm")])
        if t == 4:
            send(nx2, T.zz2[:], T.zz0[:], "z2", al("zz0"), al("zz2"))
            op("G", lambda: g.iota(T.iw[:], [[1, 4096]], 0, 0), [al("iw")], [])

    fbn = [0]

    def table(t, h):
        return ("offi%d" % (t // 4), 8 * h) if t % 4 == 0 and t > 0 else ("off", 16 * t + 8 * h)

    def p_gather(t, h):
        on, lo = table(t, h)
        op("S", lambda: S.activation(T["pb%d" % h][:], T.phw[:, 0:3840].indirect(T[on][:, lo:lo + 8]), F.Copy), [al("pb%d" % h)], [al("phw"), (on, lo, lo + 8)])

    def p_turn(h):
        vop(lambda: V.transpose(T["pt%d" % h][:], T["pb%d" % h][:]), [al("pt%d" % h)], [al("pb%d" % h)])

    def turned(h, name, mat, last):
        ps = "ps%d" % h
        for u in range(2):
            for w in range(2):
                op("P", mm(T[ps][:, 64 * u:64 * u + 64], T[mat][:, 2 * u + w], T[name][:, :, 16 * w:16 * w + 16], False, last and u == 1 and w == 1),
                   [al(ps)], [al(mat), al(name)])

    def names(t, h):
        (on, lo), nm = table(t, h), "nm%d" % h
        vop(lambda: V.tensor_copy(T[nm][:], T.adjw[:, 0:3840].indirect(T[on][:, lo:lo + 8])), [al(nm)], [al("adjw"), (on, lo, lo + 8)])

    def start(t, h, late_p=False):
        nm, dr, aa, xr, ps, nf, nt = ("%s%d" % (q, h) for q in ("nm", "dr", "aa", "xr", "ps", "nf", "nt"))
        zz, z0, n0 = "zz%d" % (t // 4), 2048 * h, 128 * h
        na = 8 - NPOS[t][h]
        m = (na + 1) // 2
        halves = [(a, b) for a, b in ((0, m), (m, na)) if a < b]
        for a, b in halves:
            vop(lambda: V.tensor_tensor(T[dr][:, 256 * a:256 * b], T.xw[:, 0:3840].indirect(T[nm][:, 16 * a:16 * b]), T[zz][:, z0 + 256 * a:z0 + 256 * b], A.subtract),
                [(dr, 256 * a, 256 * b)], [al("xw"), al(nm), al(zz)])
        soft.append(lambda: vop(lambda: V.tensor_scalar(T[nf][:], T[nm][:], 1920.0, None, A.subtract), [al(nf)], [al(nm)]))
        soft.append(lambda: vop(lambda: V.transpose(T[nt][:], T[nf][:]), [al(nt)], [al(nf)]))
        if not late_p:
            p_gather(t, h)
            soft.append(lambda: p_turn(h))

        def s_abs(a, b, src, s0):
            op("S", lambda: S.activation(T[aa][:, 16 * a:16 * b, :], T[src][:, s0:s0 + 256 * (b - a)], F.Abs), [(aa, 256 * a, 256 * b)], [(src, s0, s0 + 256 * (b - a))])
        op("P", mm(T[ps][:, 0:128], T.onesh[:], T.kc[:], True, False), [al(ps)], [al("onesh"), al("kc")])
        if t == 0:
            op("P", mm(T[ps][:, 0:128], T.idn[:], T.nts[:, n0:n0 + 128], False, False), [al(ps)], [al("idn"), al("nts")])
        else:
            for y in range(2):
                q = 2 * (t - 1) + y
                op("P", mm(T[ps][:, 0:128], T.sh[:, q, :], T.nts[:, n0 + 16 * y:n0 + 16 * y + 128], False, False), [al(ps)], [("sh", q, q + 1), al("nts")])
        fs = []
        for a in range(na, 8, 2):
            b = min(a + 2, 8)
            fb = "fb%d" % (fbn[0] % 2)
            fbn[0] += 1
            x0, x1 = 256 * (a - na), 256 * (b - na)
            op("S", lambda: S.activation(T[xr][:, x0:x1], T.xw[:, 0:3840].indirect(T[nm][:, 16 * a:16 * b]), F.Copy), [(xr, x0, x1)], [al("xw"), al(nm)])
            op("P", mm(T[fb][:, 0:x1 - x0], T.idm[:], T[zz][:, z0 + 256 * a:z0 + 256 * b], True, False), [al(fb)], [al("idm"), al(zz)])
            op("P", mm(T[fb][:, 0:x1 - x0], T.idn[:], T[xr][:, x0:x1], False, True), [al(fb)], [al("idn"), (xr, x0, x1)])
            fs.append((a, b, fb, 0))
            if len(fs) > 1 and b < 8:
                s_abs(*fs.pop(0))
        for a, b in halves:
            s_abs(a, b, dr, 256 * a)
        for q in fs:
            s_abs(*q)

    def sums(t, h, late_p=False):
        aa, ps = "aa%d" % h, "ps%d" % h
        turned(h, "nt%d" % h, "ef", False)
        if not late_p:
            turned(h, "pt%d" % h, "eb", False)
        for r in range(16):
            for u in range(2):
                op("P", mm(T[ps][:, 64 * u:64 * u + 64], T.bsl[:, 15 - r:143 - r], T[aa][:, 16 * u + r::32, :], False, (not late_p) and r == 15 and u == 1),
                   [al(ps)], [al("bsl"), al(aa)])

    def settle():
        while soft:
            fill(1)
        while pending:
            sums(*pending.pop(0))

    def finish(t, h):
        hi, sc, ni, ps = "hi%d" % (t // 4), "sc%d" % h, "ni%d" % h, "ps%d" % h
        c0, o = 16 * (t % 4) + 8 * h, 16 * (t + 1) + 8 * h
        vop(lambda: V.tensor_tensor_scan(T[sc][:], T.rst[:], T[ps][:, 0:128], 0.0, A.add, A.max), [al(sc)], [al("rst"), al(ps)])
        vop(lambda: V.tensor_copy(T[hi][:, c0:c0 + 8], T[sc][:, 15:128:16]), [(hi, c0, c0 + 8)], [al(sc)])
        vop(lambda: V.tensor_scalar(T[ni][:], T[hi][:, c0:c0 + 8], 4095, None, A.bitwise_and), [al(ni)], [(hi, c0, c0 + 8)])
        for u in range(2):
            vop(lambda: V.tensor_copy(T.off[:, o + u:o + 8:2], T[ni][:, 4 * u:4 * u + 4]), [("off", o + 4 * u, o + 4 * u + 4)], [al(ni)])
        if t in (3, 7):
            i = t // 4 + 1
            send(nxt, T["offi%d" % i][:, 8 * h:8 * h + 8], T.off[:, o:o + 8], "o%d%d" % (i, h), ("off", o, o + 8), ("offi%d" % i, 8 * h, 8 * h + 8))

    def distance(i):
        o, zz, ds = 64 * (i + 1), "zz%d" % i, "ds%d" % i
        vop(lambda: V.tensor_tensor(T.dg[:], T.xw[:, 0:3840].indirect(T.off[:, o:o + 16]), T[zz][:, 0::16], A.subtract), [al("dg")], [al("xw"), ("off", o, o + 16), al(zz)])
        op("S", lambda: S.activation(T.da[:], T.dg[:], F.Abs), [al("da")], [al("dg")])
        for r in range(16):
            op("P", mm(T.pm[:, 0:16], T.bsl[:, 15 - r:143 - r], T.da[:, :, r], r == 0, r == 15), [al("pm")], [al("bsl"), al("da")])
        op("S", lambda: S.activation(T[ds][:], T.pm[:, 0:16], F.Copy), [al(ds)], [al("pm")])
        if i > 0:
            send(prv, T["din%d" % i][:], T[ds][:], "d%d" % i, al(ds), al("din%d" % i))

    def trail(v):
        L = []
        hi, nv, uf, ud, ul, kl, dl, ubc, eq = ("%s%d" % (q, v) for q in ("hi", "nv", "uf", "ud", "ul", "kl", "dl", "ubc", "eq"))

        def c(f, w, r):
            L.append(lambda: vop(f, w, r))

        def tt(out, a, b, o, w, r):
            c(lambda: V.tensor_tensor(out, a, b, o), w, r)

        def ts(out, a, s1, s2, o1, o2, w, r):
            c(lambda: V.tensor_scalar(out, a, s1, None, o1) if s2 is None else V.tensor_scalar(out, a, s1, s2, o1, o2), w, r)
        if v == 0:
            c(lambda: V.tensor_copy(T[nv][:, 0:16], T.v0t[:]), [(nv, 0, 16)], [al("v0t")])
        else:
            for h, u in HU:
                a = 8 * h + 4 * u
                c(lambda h=h, u=u, a=a: V.tensor_copy(T[nv][:, a:a + 4], T["offi%d" % v][:, 8 * h + u:8 * h + 8:2]), [(nv, a, a + 4)], [("offi%d" % v, 8 * h, 8 * h + 8)])
        ts(T[nv][:, 16:80], T[hi][:], 4095, None, A.bitwise_and, None, [(nv, 16, 80)], [al(hi)])
        ts(T.kv[:], T[hi][:], 12, 15, A.arith_shift_right, A.bitwise_and, [al("kv")], [al(hi)])
        c(lambda: V.memset(T.al[:], 1.0), [al("al")], [])
        for d in range(1, 5):
            tt(T.ee[:, d - 1:4, 16 * (5 - d):16 * (6 - d)], T[nv][:, 0:16 * (5 - d)], T[nv][:, 16 * d:80], A.is_equal, [("ee", d, d + 1)], [al(nv)])
        ts(T.cod[:], T.kv[:], 4096.0, 65536.0, A.mult, A.add, [al("cod")], [al("kv")])
        tt(T.cod[:], T.cod[:], T[nv][:, 0:64], A.add, [al("cod")], [al("cod"), al(nv)])
        for s in range(1, 5):
            e0, n = 16 * (5 - s), 16 * (s - 1)
            if s == 1:
                c(lambda: V.tensor_copy(T.hh[:, 0:16], T.ee[:, 0, 64:80]), [("hh", 0, 16)], [al("ee")])
            else:
                tt(T.hh[:, 0:n], T.al[:, 0:n], T.ee[:, s - 1, e0:e0 + n], A.mult, [("hh", 0, n)], [al("al"), al("ee")])
                for q in range(16, n, 16):
                    tt(T.hh[:, q:q + 16], T.hh[:, q - 16:q], T.hh[:, q:q + 16], A.add, [("hh", q, q + 16)], [("hh", q - 16, q + 16)])
                tt(T.hh[:, n:n + 16], T.hh[:, n - 16:n], T.ee[:, s - 1, 64:80], A.add, [("hh", n, n + 16)], [("hh", n - 16, n), al("ee")])
            tt(T.al[:, 0:16 * s], T.al[:, 0:16 * s], T.hh[:, 0:16 * s], A.is_gt, [("al", 0, 16 * s)], [al("al"), ("hh", 0, 16 * s)])
        c(lambda: V.memset(T.pl[:, 0:16], 0.0), [("pl", 0, 16)], [])
        for q in (16, 32, 48):
            tt(T.pl[:, q:q + 16], T.pl[:, q - 16:q], T.al[:, q - 16:q], A.add, [("pl", q, q + 16)], [("pl", q - 16, q), al("al")])
        ts(T.na[:], T.al[:], -9.0, 9.0, A.mult, A.add, [al("na")], [al("al")])
        tt(T.pl[:], T.pl[:], T.na[:], A.add, [al("pl")], [al("pl"), al("na")])
        for p in range(4):
            ts(T.ww[:, p, :], T.pl[:], float(p), None, A.is_equal, None, [("ww", p, p + 1)], [al("pl")])
        for p in range(4):
            tt(T.w2[:, p], T.ww[:, p, :], T.cod[:], A.mult, [("w2", p, p + 1)], [("ww", p, p + 1), al("cod")])
        tt(T.w3[:], T.w2[:, :, 0:2, :], T.w2[:, :, 2:4, :], A.add, [al("w3")], [al("w2")])
        tt(T.cp[:], T.w3[:, :, 0, :], T.w3[:, :, 1, :], A.add, [al("cp")], [al("w3")])
        c(lambda: V.tensor_copy(T.ci[:], T.cp[:]), [al("ci")], [al("cp")])
        ts(T.nx[:], T.cp[:], 0.0, None, A.is_equal, None, [al("nx")], [al("cp")])
        tt(T.nx[:], T.nx[:], T.dum[:], A.mult, [al("nx")], [al("nx"), al("dum")])
        ts(T.kv[:], T.ci[:], 12, 15, A.arith_shift_right, A.bitwise_and, [al("kv")], [al("ci")])
        ts(T.ci[:], T.ci[:], 4095, None, A.bitwise_and, None, [al("ci")], [al("ci")])
        tt(T[uf][:], T.ci[:], T.nx[:], A.add, [al(uf)], [al("ci"), al("nx")])
        c(lambda: V.tensor_copy(T[ul][:], T[uf][:]), [al(ul)], [al(uf)])
        tt(T[ud][:], T[uf][:], T.dum[:], A.subtract, [al(ud)], [al(uf), al("dum")])
        ts(T[kl][:], T.kv[:], -1.0, 15.0, A.mult, A.add, [al(kl)], [al("kv")])
        for p in range(4):
            L.append(lambda p=p: op("S", lambda: S.activation(T[dl][:, 256 * p:256 * p + 256], T.dwin[:, 0:16].indirect(T[kl][:, 16 * p:16 * p + 16]), F.Copy),
                                    [(dl, 256 * p, 256 * p + 256)], [al("dwin"), al(kl)]))
            c(lambda p=p: V.tensor_copy(T[ubc][:, 256 * p:256 * p + 256], T.iw[:, 0:4096].indirect(T[ul][:, 16 * p:16 * p + 16])), [(ubc, 256 * p, 256 * p + 256)], [al("iw"), al(ul)])
            for q in range(16 * p, 16 * p + 16):
                j, a = q % 8, 128 * (q // 8)
                ts(T[eq][:, q, 0:128 - 16 * j], T[ubc][:, a + 16 * j:a + 128], T[uf][:, q:q + 1], None, A.is_equal, None, [(eq, 128 * q, 128 * q + 128)], [(ubc, a, a + 128), al(uf)])
        for x in range(16):
            L.append(lambda x=x: op("S", lambda: S.activation(T[eq][:, :, x], T[eq][:, :, x], F.Copy, scale=T.mw[:, x:x + 1]), [al(eq)], [al(eq), al("mw")]))
        return L

    def better(v, third):
        eq, din, ds = "eq%d" % v, "din%d" % (v + 1), "ds%d" % v
        vop(lambda: V.tensor_tensor(T.bet[:], T[din][:], T[ds][:], A.is_gt), [al("bet")], [al(din), al(ds)])
        for c in range(16):
            pos = 8 * (c // 8) + 2 * (c % 4) + (c % 8) // 4
            if c % 3 != third:
                vop(lambda: V.tensor_scalar(T.bt[:, c, :], T.bm[:], T.bet[:, pos:pos + 1], None, A.mult), [("bt", c, c + 1)], [al("bm"), al("bet")])
            else:
                op("S", lambda: S.activation(T.bt[:, c, :], T.bm[:], F.Copy, scale=T.bet[:, pos:pos + 1]), [("bt", c, c + 1)], [al("bm"), al("bet")])
        for p in range(4):
            cn, base = BANK[p]
            if base == 0:
                n = 2 if p == 1 else 1
                op("P", mm(T[cn][:, 0:256 * n], T.idn[:], T.pen[:, 0:16 * n, :], True, False), [al(cn)], [al("idn"), al("pen")])
            for c in range(16):
                j, q, o = c % 8, 16 * p + c, base + 128 * (c // 8)
                op("P", mm(T[cn][:, o + 16 * j:o + 128], T.bt[:, c, :], T[eq][:, q, 0:128 - 16 * j], False, c == 15 and p != 1),
                   [al(cn)], [("bt", c, c + 1), (eq, 128 * q, 128 * q + 128)])

    def chain(v):
        ud, dl = "ud%d" % v, "dl%d" % v
        for p in range(4):
            if p < 2:
                o, n = (0, 16) if p == 0 else (16, 48)
                for cn, s0, w in ([("cn0", 0, 256)] if p == 0 else [("cn1", 0, 512), ("cn2", 512, 256)]):
                    vop(lambda: V.tensor_tensor_scan(T.scn[:, s0:s0 + w], T.rsp[:, 0:w], T[cn][:, 0:w], 1.0e6, A.add, A.min), [("scn", s0, s0 + w)], [al("rsp"), al(cn)])
                vop(lambda: V.tensor_scalar(T.okm[:, 0:n], T.scn[:, 15:16 * n:16], 0.5, None, A.is_equal), [al("okm")], [al("scn")])
                vop(lambda: V.tensor_tensor(T.okm[:, 0:n], T.okm[:, 0:n], T[ud][:, o:o + n], A.mult), [al("okm")], [al("okm"), al(ud)])
                vop(lambda: V.tensor_tensor(T.okm[:, 0:n], T.okm[:, 0:n], T.dum[:, o:o + n], A.add), [al("okm")], [al("okm"), al("dum")])
                vop(lambda: V.tensor_copy(T.ofl[:, o:o + n], T.okm[:, 0:n]), [("ofl", o, o + n)], [al("okm")])
            vop(lambda: V.tensor_tensor(T.t1[:], T.phw[:, 0:4096].indirect(T.ofl[:, 16 * p:16 * p + 16]), T[dl][:, 256 * p:256 * p + 256], A.add),
                [al("t1")], [al("phw"), ("ofl", 16 * p, 16 * p + 16), (dl, 256 * p, 256 * p + 256)])
            vop(lambda: V.tensor_scalar(T.t2[:], T.t1[:], 0.0, 20.0, A.max, A.min), [al("t2")], [al("t1")])
            for h in (1, 0):
                vop(lambda: V.tensor_copy(T.phw[:, 0:4096].indirect(T.ofl[:, 16 * p + 8 * h:16 * p + 8 * h + 8]), T.t2[:, 128 * h:128 * h + 128]),
                    [al("phw")], [al("t2"), ("ofl", 16 * p, 16 * p + 16)])

    for t in range(12):
        if t in (4, 8):
            v = t // 4 - 1
            finish(t - 1, 0)
            settle()
            fill(KEEP)
            finish(t - 1, 1)
            if v == 1:
                distance(1)
            fill(len(queue))
            queue.extend(trail(v))
            if v == 0:
                queue.insert(20, lambda: distance(0))
        if t == 8:
            names(8, 0)
            start(8, 0, True)
            names(8, 1)
            fill(FR[0])
            better(0, 9)
            while soft:
                fill(1)
            sums(8, 0, True)
            start(8, 1, True)
            while soft:
                fill(1)
            sums(8, 1, True)
            fill(FR[1])
            chain(0)
            for h in range(2):
                p_gather(8, h)
                p_turn(h)
                turned(h, "pt%d" % h, "eb", True)
            continue
        for h in range(2):
            n = len(queue)
            if t % 4:
                finish(t - 1, h)
            names(t, h)
            settle()
            start(t, h)
            pending.append((t, h))
            if t > 3:
                left = 2 * (4 - t % 4) - h
                fill(max(0, -(-(n - (KEEP if t < 8 else 0)) // left) - n + len(queue) + len(soft)))
    fill(len(queue) + len(soft))
    finish(11, 0)
    settle()
    finish(11, 1)
    distance(2)
    vop(lambda: V.tensor_scalar(T.yvi[:], T.hi2[:, 48:64], 4095, None, A.bitwise_and), [al("yvi")], [("hi2", 48, 64)])
    vop(lambda: V.tensor_copy(T.yvt[:], T.yvi[:]), [al("yvt")], [al("yvi")])
    op("Y", lambda: g.sync.dma_start(T.yv[:], T.yvt[:]), [], [al("yvt")], "ov", 16)
    better(1, 2)
    chain(1)
    op("Y", lambda: g.sync.dma_start(T.yp[:, 0:1920], T.phw[:, 0:1920]), [], [("phw", 0, 1920)], "oy0", 16)
    op("S", lambda: g.scalar.dma_start(T.yp[:, 1920:3840], T.phw[:, 1920:3840]), [], [("phw", 1920, 3840)], "oy1", 16)
    for s, v in cnt.items():
        if v:
            need("G", (s, v))
